import numpy as np
import ml_dtypes


def mxq(x, axis, fmt="e4m3"):
    dtype, down = {"e4m3": (ml_dtypes.float8_e4m3fn, 7), "e5m2": (ml_dtypes.float8_e5m2, 14)}[fmt]
    v = np.moveaxis(np.asarray(x, np.float32).astype(ml_dtypes.bfloat16).astype(np.float64), axis, -1)
    blocks = v.reshape(v.shape[:-1] + (-1, 32))
    amax = np.abs(blocks).max(-1, keepdims=True)
    byte = np.maximum(np.where(amax > 0, np.frexp(amax)[1] - 1 + 127, 0) - down, 1)
    scale = np.exp2(byte - 127.0)
    codes = (blocks / scale).astype(np.float32).astype(dtype).astype(np.float64)
    return np.moveaxis((codes * scale).reshape(v.shape), -1, axis)


WIDE = False


def mx_kscale(k):
    if not WIDE:
        return np.ones(k)
    levels = np.array([10, -10, 5, -5, 0])
    if k % 512:
        return np.exp2(np.random.permutation(np.resize(levels, k // 32))).repeat(32)
    a = np.empty((k // 512, 16))
    for p in range(k // 512):
        a[p, :8] = np.random.permutation(np.resize(levels, 8))
        for g in range(8):
            far = levels[np.abs(levels - a[p, g]) >= 10]
            a[p, g + 8] = far[np.random.randint(len(far))]
    return np.exp2(a.ravel()).repeat(32)


BF16 = ml_dtypes.bfloat16


def bf(x):
    return np.asarray(x, np.float32).astype(BF16)


def f64(x):
    return np.asarray(x).astype(np.float64)


E2M1 = np.array([0.0, 0.5, 1.0, 1.5, 2.0, 3.0, 4.0, 6.0, -0.0, -0.5, -1.0, -1.5, -2.0, -3.0, -4.0, -6.0])


def pack_weight(w, fmt):
    k, n = w.shape
    w = f64(bf(w)).reshape(k // 32, 32, n)
    amax = np.abs(w).max(1)
    if fmt == "e4m3":
        byte = np.frexp(amax)[1] - 1 + 127 - 7
    else:
        mant, ex = np.frexp(amax / 6.0)
        byte = np.where(mant > 0.5, ex, ex - 1) + 127
    byte = np.clip(np.where(amax > 0, byte, 1), 1, 254)
    scaled = (w * np.exp2(127.0 - byte)[:, None, :]).reshape(k, n).astype(np.float32)
    by_word = np.ascontiguousarray(scaled.reshape(k // 512, 128, 4, n).transpose(0, 1, 3, 2))
    if fmt == "e4m3":
        words = by_word.astype(ml_dtypes.float8_e4m3fn).view(np.uint8)
    else:
        c = by_word.astype(ml_dtypes.float4_e2m1fn).view(np.uint8) & 0xF
        words = c[..., 0::2] | (c[..., 1::2] << 4)
    return np.ascontiguousarray(words), np.ascontiguousarray(byte.astype(np.uint8).reshape(k // 512, 16, n))


def unpack_weight(words, scales, fmt):
    g, p, n, _ = words.shape
    if fmt == "e4m3":
        vals = np.ascontiguousarray(words).view(ml_dtypes.float8_e4m3fn).astype(np.float64)
    else:
        nib = np.empty((g, p, n, 4), np.uint8)
        nib[..., 0::2] = words & 0xF
        nib[..., 1::2] = words >> 4
        vals = E2M1[nib]
    vals = vals * np.repeat(np.exp2(scales.astype(np.float64) - 127.0), 8, axis=1)[..., None]
    return vals.transpose(0, 1, 3, 2).reshape(g * 512, n)
def pack4(w):
    words, scales = pack_weight(w, "e2m1")
    return words.reshape(words.shape[0], 128, -1), scales


def unpack4(words, scales):
    return unpack_weight(words.reshape(words.shape[0], 128, -1, 2), scales, "e2m1")


M, D, H = 1024, 2048, 512


def setup_inputs():
    s, u, t = mx_kscale(H), mx_kscale(M), mx_kscale(D)
    w = np.random.standard_normal((D, H)) / (3.0 * np.sqrt(H))
    wd_words, wd_scales = pack4(w.T / s[:, None] * t)
    wb_words, wb_scales = pack4(w / t[:, None])
    pt = np.random.standard_normal((M, M)) / (3.0 * np.sqrt(M))
    pt_words, pt_scales = pack4(pt / u[:, None])
    return {"x": bf(np.random.standard_normal((M, D)) * u[:, None] * t),
            "c": bf(np.random.standard_normal((M, H)) * u[:, None] * s),
            "wd_words": wd_words, "wd_scales": wd_scales,
            "pt_words": pt_words, "pt_scales": pt_scales,
            "wb_words": wb_words, "wb_scales": wb_scales,
            "a": bf((1 + 0.1 * np.random.standard_normal(M)) / u),
            "rate": bf(1 + 0.1 * np.random.standard_normal(H))}


def reference(x, c, wd_words, wd_scales, pt_words, pt_scales, wb_words, wb_scales, a, rate):
    wd = unpack4(wd_words, wd_scales)
    pt = unpack4(pt_words, pt_scales)
    wb = unpack4(wb_words, wb_scales)
    e = f64(x) - (mxq(f64(c), 1, "e4m3") @ wd)
    f = f64(a)[:, None] * e + (pt.T @ mxq(e, 0, "e4m3"))
    return f64(rate) * (mxq(f, 1, "e4m3") @ wb)

from contextlib import ExitStack

import concourse.mybir as mybir
from concourse.masks import make_identity

M, D, H = 1024, 2048, 512
FLOPS = 2 * (M * H * D + M * M * D + M * D * H)

F32 = mybir.dt.float32
BF16 = mybir.dt.bfloat16
I32 = mybir.dt.int32
U32 = mybir.dt.uint32
U8 = mybir.dt.uint8
E4M3X4 = mybir.dt.float8_e4m3fn_x4
E2M1X4 = mybir.dt.float4_e2m1fn_x4
ALU = mybir.AluOpType

P = 128
N = 512
CHUNKS = D // N
HALVES = 2 * CHUNKS
SLOTS = 4


def tile_tied_autoencoder_code_step_t2_kernel(
    tc, x, c, wd_words, wd_scales, pt_words, pt_scales, wb_words, wb_scales, a, rate, out
):
    nc = tc.nc
    with ExitStack() as ctx:
        keep = ctx.enter_context(tc.tile_pool(name="keep", bufs=1))
        work = ctx.enter_context(tc.tile_pool(name="work", bufs=2))
        psum = ctx.enter_context(tc.psum_pool(name="psum", bufs=1))
        ctx.enter_context(tc.manual_schedule())

        ident = keep.tile([P, P], F32, name="ident")
        warm = keep.tile([P, 2], F32, name="warm")
        c_raw = [keep.tile([P, 2, H], BF16, name="c_raw%d" % k) for k in range(4)]
        c_codes = keep.tile([P, M], U32, name="c_codes", align_bytes=64)
        c_planes = keep.tile([P, M], U8, name="c_planes", align_bytes=64)
        x_sb = [keep.tile([P, SLOTS, N], BF16, name="x_sb%d" % s) for s in range(HALVES)]
        wd_sb = keep.tile([P, 2 * D], U8, name="wd_sb", align_bytes=64)
        wd_pl = keep.tile([P, D], U8, name="wd_pl", align_bytes=64)
        pt_raw = keep.tile([P, 2, 2 * M], U8, name="pt_raw", align_bytes=64)
        pt_sb = keep.tile([P, 2, 2 * M], U8, name="pt_sb", align_bytes=64)
        pt_plraw = keep.tile([P, 2, M], U8, name="pt_plraw", align_bytes=64)
        pt_pl = keep.tile([P, 2, M], U8, name="pt_pl", align_bytes=64)
        wb_sb = keep.tile([P, CHUNKS, 2 * H], U8, name="wb_sb", align_bytes=64)
        wb_pl = keep.tile([P, CHUNKS, H], U8, name="wb_pl", align_bytes=64)
        a_sb = keep.tile([P, 2, SLOTS], BF16, name="a_sb")
        rate_sb = keep.tile([P, H], BF16, name="rate_sb")
        f_codes = [keep.tile([P, N], U32, name="f_codes%d" % h, align_bytes=64) for h in range(HALVES)]
        f_planes = [keep.tile([P, N], U8, name="f_planes%d" % h, align_bytes=64) for h in range(HALVES)]

        c_view = c.rearrange("(g p t) k -> g p t k", p=P, t=SLOTS)
        x_view = x.rearrange("(g p t) d -> g p t d", p=P, t=SLOTS)
        out_view = out.rearrange("(g p t) h -> g p t h", p=P, t=SLOTS)

        def load_c(k):
            nc.sync.dma_start(out=c_raw[k][:], in_=c_view[k // 2][:, 2 * (k % 2) : 2 * (k % 2) + 2, :])

        def load_x(s):
            nc.sync.dma_start(out=x_sb[s][:], in_=x_view[s % 2][:, :, N * (s // 2) : N * (s // 2 + 1)])

        def load_wd(lo, hi):
            nc.sync.dma_start(
                out=wd_sb[:, 2 * lo : 2 * hi].bitcast(I32), in_=wd_words[0][:, 2 * lo : 2 * hi].bitcast(I32)
            )

        nc.gpsimd.memset(warm[:], 0.0)
        make_identity(nc, ident[:])
        nc.scalar.copy(out=warm[:, 1:2], in_=warm[:, 0:1])

        nc.vector.memset(wd_pl[:].bitcast(I32), 0)
        nc.vector.memset(pt_plraw[:].rearrange("p g n -> p (g n)").bitcast(I32), 0)
        nc.vector.memset(wb_pl[:].rearrange("p g n -> p (g n)").bitcast(I32), 0)

        load_c(0)
        load_c(1)
        for r in range(4):
            queue = nc.scalar if r < 2 else nc.gpsimd
            queue.dma_start(out=wd_pl[r:P:32, :].bitcast(I32), in_=wd_scales[0][r:16:4, :].bitcast(I32))
        load_wd(0, N)
        load_x(0)
        for g in range(2):
            nc.sync.dma_start(out=pt_raw[:, g, :].bitcast(I32), in_=pt_words[g].bitcast(I32))
        load_c(2)
        load_c(3)
        load_x(1)
        for r in range(4):
            nc.sync.dma_start(
                out=pt_plraw[r:P:32, :, :].bitcast(I32),
                in_=pt_scales[:, r:16:4, :].rearrange("g q n -> q g n").bitcast(I32),
            )
        for r in range(4):
            nc.sync.dma_start(
                out=wb_pl[r:P:32, :, :].bitcast(I32),
                in_=wb_scales[:, r:16:4, :].rearrange("g q n -> q g n").bitcast(I32),
            )
        load_wd(N, D)
        nc.sync.dma_start(out=a_sb[:], in_=a.rearrange("(g p t) -> p g t", p=P, t=SLOTS))
        for s in range(2, HALVES):
            load_x(s)
            if s == 3:
                nc.sync.dma_start(
                    out=wb_sb[:].bitcast(I32), in_=wb_words.rearrange("g p w -> p g w").bitcast(I32)
                )
        nc.sync.dma_start(out=rate_sb[:], in_=rate.partition_broadcast(P))

        counts = {"m": 0, "t": 0}
        depth = {"m": 3, "t": 2}

        def bank(kind):
            k = counts[kind] % depth[kind]
            counts[kind] += 1
            b = psum.tile([P, N], F32, name="%s%d" % (kind, k), tag="%s%d" % (kind, k))
            return b

        def turn_c(k):
            turned = bank("t")
            for i in range(2):
                words = c_raw[k][:, i, :].bitcast(F32)
                for u in range(2):
                    lo = P * (2 * i + u)
                    nc.tensor.transpose(turned[:, lo : lo + P], words[:, u : 2 * P : 2], ident[:])
            c_grp = work.tile([P, 4 * 2 * P], BF16, name="c_grp", align_bytes=64)
            nc.scalar.copy(
                out=c_grp[:].bitcast(F32).rearrange("p (i r u) -> p i r u", i=2, u=2),
                in_=turned[:].rearrange("p (i u r) -> p i r u", i=2, u=2),
            )
            return c_grp

        def quantize_c(k, c_grp):
            cols = slice(2 * P * k, 2 * P * (k + 1))
            nc.vector.quantize_mx(out=c_codes[:, cols].bitcast(E4M3X4), scales=c_planes[:, cols], in_=c_grp[:])

        def permute_pt(g, j):
            nc.vector.tensor_copy(
                out=pt_sb[:, g, 1024 * j : 1024 * (j + 1)].rearrange("p (t m b) -> p t m b", t=4, b=2),
                in_=pt_raw[:, g, 1024 * j : 1024 * (j + 1)].rearrange("p (m t b) -> p t m b", t=4, b=2),
            )

        def permute_pt_scales(g):
            nc.vector.tensor_copy(
                out=pt_pl[:, g, :].rearrange("p (j t m) -> p j t m", j=2, t=4),
                in_=pt_plraw[:, g, :].rearrange("p (j m t) -> p j t m", j=2, t=4),
            )

        e32 = {}
        e_codes = {}
        e_planes = {}
        e_grp = {}
        f_sb = {}
        f_grp = {}
        e_bank = {}

        def e_matmul(s, t):
            ch, g = divmod(s, 2)
            b = bank("m")
            e_bank[(s, t)] = b
            rows = slice(P * (4 * g + t), P * (4 * g + t + 1))
            nc.tensor.matmul_mx(
                out=b[:],
                lhsT=c_codes[:, rows].bitcast(E4M3X4),
                lhsT_scale=c_planes[:, rows],
                rhs=wd_sb[:, 2 * N * ch : 2 * N * (ch + 1)].bitcast(E2M1X4),
                rhs_scale=wd_pl[:, N * ch : N * (ch + 1)],
                start=True,
                stop=True,
            )

        def e_subtract(s, t):
            if t == 0:
                e32[s] = work.tile([P, SLOTS, N], F32, name="e32", bufs=4)
            b = e_bank.pop((s, t))
            nc.vector.tensor_tensor(
                out=e32[s][:, t, :].rearrange("p (u m e) -> p u m e", u=2, e=2),
                in0=x_sb[s][:, t, :].rearrange("p (m u e) -> p u m e", u=2, e=2),
                in1=b[:].rearrange("p (m u e) -> p u m e", u=2, e=2),
                op=ALU.subtract,
            )

        def e_group(s):
            e_grp[s] = work.tile([P, N, SLOTS], BF16, name="e_grp", bufs=2, align_bytes=64)
            for k in range(2):
                cols = slice(N // 2 * k, N // 2 * (k + 1))
                nc.scalar.copy(
                    out=e_grp[s][:, cols, :].rearrange("p (n i) t -> p n t i", i=4),
                    in_=e32[s][:, :, cols].rearrange("p t (n i) -> p n t i", i=4),
                )

        def e_quantize(s):
            e_codes[s] = work.tile([P, N], U32, name="e_codes", bufs=4, align_bytes=64)
            e_planes[s] = work.tile([P, N], U8, name="e_planes", bufs=4, align_bytes=64)
            nc.vector.quantize_mx(
                out=e_codes[s][:].bitcast(E4M3X4),
                scales=e_planes[s][:],
                in_=e_grp[s][:].rearrange("p n t -> p (n t)"),
            )

        def f_tile(h, t):
            ch, g = divmod(h, 2)
            if t == 0:
                f_sb[h] = work.tile([P, SLOTS, N], BF16, name="f_sb", bufs=2)
            b = bank("m")
            tile_no = 4 * g + t
            for k in range(2):
                nc.tensor.matmul_mx(
                    out=b[:],
                    lhsT=pt_sb[:, k, 2 * P * tile_no : 2 * P * (tile_no + 1)].bitcast(E2M1X4),
                    lhsT_scale=pt_pl[:, k, P * tile_no : P * (tile_no + 1)],
                    rhs=e_codes[2 * ch + k][:].bitcast(E4M3X4),
                    rhs_scale=e_planes[2 * ch + k][:],
                    start=(k == 0),
                    stop=(k == 1),
                )
            nc.vector.scalar_tensor_tensor(
                out=f_sb[h][:, t, :],
                in0=e32[h][:, t, :],
                scalar=a_sb[:, g, t : t + 1],
                in1=b[:],
                op0=ALU.mult,
                op1=ALU.add,
            )

        def f_turn(h, pair):
            if pair == 0:
                f_grp[h] = work.tile([P, SLOTS * P * 4], BF16, name="f_grp", bufs=2, align_bytes=64)
            turned = bank("t")
            for i in range(2):
                words = f_sb[h][:, 2 * pair + i, :].bitcast(F32)
                for u in range(2):
                    lo = P * (2 * i + u)
                    nc.tensor.transpose(turned[:, lo : lo + P], words[:, P * u : P * (u + 1)], ident[:])
            half = slice(1024 * pair, 1024 * (pair + 1))
            nc.scalar.copy(
                out=f_grp[h][:, half].bitcast(F32).rearrange("p (i r u) -> p i r u", i=2, u=2),
                in_=turned[:].rearrange("p (i u r) -> p i r u", i=2, u=2),
            )

        def f_quantize(h, lo, hi):
            nc.vector.quantize_mx(
                out=f_codes[h][:, P * lo : P * hi].bitcast(E4M3X4),
                scales=f_planes[h][:, P * lo : P * hi],
                in_=f_grp[h][:, 4 * P * lo : 4 * P * hi],
            )

        o_bank = {}

        def o_pass(n, ch, tag):
            if ch == 0:
                o_new = psum.tile([P, N], F32, name="o", tag=tag)
                o_bank[n] = o_new
            g, t = divmod(n, 4)
            h = 2 * ch + g
            nc.tensor.matmul_mx(
                out=o_bank[n][:],
                lhsT=f_codes[h][:, P * t : P * (t + 1)].bitcast(E4M3X4),
                lhsT_scale=f_planes[h][:, P * t : P * (t + 1)],
                rhs=wb_sb[:, ch, :].bitcast(E2M1X4),
                rhs_scale=wb_pl[:, ch, :],
                start=(ch == 0),
                stop=(ch == CHUNKS - 1),
            )

        def o_store(n):
            g, t = divmod(n, 4)
            o_sb = work.tile([P, H], F32, name="o_sb", bufs=4)
            nc.vector.tensor_tensor(out=o_sb[:], in0=o_bank[n][:], in1=rate_sb[:], op=ALU.mult)
            nc.sync.dma_start(out=out_view[g][:, t, :], in_=o_sb[:])

        grp = turn_c(0)
        quantize_c(0, grp)
        grp = turn_c(1)
        quantize_c(1, grp)

        tags = ["o0", "o1", "o2", "m2"]
        for s in range(HALVES + 2):
            h = s - 2
            if s < HALVES:
                e_matmul(s, 0)
                e_matmul(s, 1)
                e_subtract(s, 0)
                e_subtract(s, 1)
            if h >= 1:
                f_turn(h - 1, 0)
                f_turn(h - 1, 1)
            if 1 <= s <= HALVES:
                e_quantize(s - 1)
            if s < HALVES:
                for t in (2, 3):
                    e_matmul(s, t)
                    e_subtract(s, t)
            if s == 0:
                permute_pt(0, 0)
                permute_pt(0, 1)
                for k in (2, 3):
                    grp = turn_c(k)
                    quantize_c(k, grp)
                permute_pt(1, 0)
            if s == 1:
                permute_pt(1, 1)
                permute_pt_scales(0)
                permute_pt_scales(1)
            if s < HALVES:
                e_group(s)
            if h >= 1:
                f_quantize(h - 1, 0, 4)
            if s == HALVES:
                depth["m"] = 2
                counts["m"] = 0
            if h >= 0:
                for t in range(4):
                    f_tile(h, t)
            if h >= 1 and (h - 1) % 2 == 0:
                ch = (h - 1) // 2
                for n in range(3):
                    o_pass(n, ch, tags[n])
            if s == HALVES:
                for ch in range(3):
                    o_pass(3, ch, tags[3])
            if s == HALVES + 1:
                o_pass(3, 3, tags[3])
                for n in range(4):
                    o_store(n)
        last = HALVES - 1
        f_turn(last, 0)
        for n in (4, 5):
            for ch in range(3):
                o_pass(n, ch, tags[n - 4])
        f_turn(last, 1)
        f_quantize(last, 0, 2)
        for n in (6, 7):
            for ch in range(3):
                o_pass(n, ch, tags[n - 4])
        f_quantize(last, 2, 4)
        for n in range(4, 8):
            o_pass(n, 3, tags[n - 4])
            o_store(n)
